import numpy as np
import ml_dtypes

BF16 = ml_dtypes.bfloat16


def bf(x):
    return np.asarray(x, np.float32).astype(BF16)


def f32(x):
    return np.asarray(x, np.float32)


def f64(x):
    return np.asarray(x).astype(np.float64)


def striped(idx):
    return np.tile(idx.reshape(-1, 16).T, (8, 1))


S, K, H, M, N, E, Q = 256, 256, 128, 512, 256, 1, 256


def gelu_tanh(v):
    return 0.5 * v * (1.0 + np.tanh(np.sqrt(2.0 / np.pi) * (v + 0.044715 * v**3)))


def setup_inputs():
    return {"base": bf(np.random.standard_normal((M, S))), "x": bf(np.random.standard_normal((K, N))), "w": bf(np.random.standard_normal((E, K, H)) / np.sqrt(K)), "b": f32(0.5 * np.random.standard_normal((H, E))), "w2": bf(1.5 * np.random.standard_normal((E, H, M)) / np.sqrt(H)), "offs": striped(np.random.permutation(S))}


def reference(base, x, w, b, w2, offs):
    idx = offs[:16].T.reshape(-1)
    z = f64(base).copy()
    for e in range(E):
        t = f64(w)[e].T @ f64(x)[:, e * Q : (e + 1) * Q] + f64(b)[:, e : e + 1]
        t = gelu_tanh(t)
        z[:, idx[e * Q : (e + 1) * Q]] += f64(w2)[e].T @ t
    return z

@@ -1,0 +1,73 @@
+import concourse.mybir as mybir
+from concourse.masks import make_identity
+
+BF16, F32, U16 = mybir.dt.bfloat16, mybir.dt.float32, mybir.dt.uint16
+GELU_TANH = mybir.ActivationFunctionType.Gelu_apprx_tanh
+
+P = 128
+K, H, M, N = 256, 128, 512, 256
+FEATURE_BLOCKS = M // P
+K_BLOCKS = K // P
+
+FLOPS = 2 * K * H * N + 2 * H * M * N
+
+
+def tile_rows_ffnback_gelu_kernel(tc, base, x, w, b, w2, offs, out):
+    nc = tc.nc
+    with (
+        tc.tile_pool(name="held", bufs=1) as held,
+        tc.psum_pool(name="psum", bufs=1) as psum,
+    ):
+        x_tile = held.tile([P, K_BLOCKS * N], BF16)
+        w_tile = held.tile([P, K_BLOCKS * H], BF16)
+        bias = held.tile([P, 1], F32)
+        base_tile = held.tile([P, FEATURE_BLOCKS, N], BF16)
+        offsets = held.tile([P, N // 16], U16)
+        w2_tile = held.tile([P, M], BF16)
+        nc.sync.dma_start(x_tile[:], x.rearrange("(p a) n -> p (a n)", a=K_BLOCKS))
+        nc.sync.dma_start(w_tile[:], w[0].rearrange("(p a) h -> p (a h)", a=K_BLOCKS))
+        nc.sync.dma_start(base_tile[:], base.rearrange("(f p) n -> p f n", p=P))
+        nc.sync.dma_start(w2_tile[:], w2[0])
+        nc.sync.dma_start(offsets[:], offs)
+        nc.scalar.dma_start(bias[:], b)
+
+        zero_column = held.tile([P, 1], F32)
+        gelu_of_zero = held.tile([P, 1], F32)
+        nc.vector.memset(zero_column[:], 0.0)
+        nc.scalar.activation(gelu_of_zero[:], zero_column[:], GELU_TANH)
+
+        identity = held.tile([P, P], BF16)
+        make_identity(nc, identity[:])
+
+        hidden_sum = psum.tile([P, N], F32)
+        for a in range(K_BLOCKS):
+            nc.tensor.matmul(
+                hidden_sum[:],
+                w_tile[:, a * H : (a + 1) * H],
+                x_tile[:, a * N : (a + 1) * N],
+                start=a == 0,
+                stop=a == K_BLOCKS - 1,
+            )
+        hidden = held.tile([P, N], BF16)
+        nc.scalar.activation(hidden[:], hidden_sum[:], GELU_TANH, bias=bias[:])
+
+        windows = [psum.tile([P, N], F32, name=f"window{f}") for f in range(FEATURE_BLOCKS)]
+        for f in range(FEATURE_BLOCKS):
+            nc.tensor.matmul(windows[f][:], identity[:], base_tile[:, f, :], start=True, stop=False)
+
+        for f in range(FEATURE_BLOCKS):
+            nc.tensor.matmul(
+                windows[f][:].indirect(offsets[:]),
+                w2_tile[:, f * P : (f + 1) * P],
+                hidden[:],
+                start=False,
+                stop=True,
+            )
+
+        for f in range(FEATURE_BLOCKS):
+            result = held.tile([P, N], F32, name=f"result{f}")
+            if f % 2 == 0:
+                nc.vector.tensor_copy(result[:], windows[f][:])
+            else:
+                nc.scalar.copy(result[:], windows[f][:])
+            nc.sync.dma_start(out[f * P : (f + 1) * P, :], result[:])

@@ -8,6 +8,8 @@ P = 128
 K, H, M, N = 256, 128, 512, 256
 FEATURE_BLOCKS = M // P
 K_BLOCKS = K // P
+WARM_UP_COLUMNS = 512
+WARM_UP_MATMULS = 4
 
 FLOPS = 2 * K * H * N + 2 * H * M * N
 
@@ -31,10 +33,13 @@ def tile_rows_ffnback_gelu_kernel(tc, base, x, w, b, w2, offs, out):
         nc.sync.dma_start(offsets[:], offs)
         nc.scalar.dma_start(bias[:], b)
 
-        zero_column = held.tile([P, 1], F32)
-        gelu_of_zero = held.tile([P, 1], F32)
-        nc.vector.memset(zero_column[:], 0.0)
-        nc.scalar.activation(gelu_of_zero[:], zero_column[:], GELU_TANH)
+        zeros = held.tile([P, WARM_UP_COLUMNS], BF16)
+        nc.vector.memset(zeros[:], 0.0)
+        gelu_of_zero = held.tile([P, 1], BF16)
+        nc.scalar.activation(gelu_of_zero[:], zeros[:, 0:1], GELU_TANH)
+        warm_up = psum.tile([P, WARM_UP_COLUMNS], F32)
+        for unused in range(WARM_UP_MATMULS):
+            nc.tensor.matmul(warm_up[:], zeros[:, 0:P], zeros[:], start=True, stop=True)
 
         identity = held.tile([P, P], BF16)
         make_identity(nc, identity[:])

@@ -8,8 +8,8 @@ P = 128
 K, H, M, N = 256, 128, 512, 256
 FEATURE_BLOCKS = M // P
 K_BLOCKS = K // P
-WARM_UP_COLUMNS = 512
-WARM_UP_MATMULS = 4
+WARM_UP_COLUMNS = 256
+WARM_UP_MATMULS = 8
 
 FLOPS = 2 * K * H * N + 2 * H * M * N
 
@@ -28,7 +28,9 @@ def tile_rows_ffnback_gelu_kernel(tc, base, x, w, b, w2, offs, out):
         w2_tile = held.tile([P, M], BF16)
         nc.sync.dma_start(x_tile[:], x.rearrange("(p a) n -> p (a n)", a=K_BLOCKS))
         nc.sync.dma_start(w_tile[:], w[0].rearrange("(p a) h -> p (a h)", a=K_BLOCKS))
-        nc.sync.dma_start(base_tile[:], base.rearrange("(f p) n -> p f n", p=P))
+        base_blocks = base.rearrange("(f p) n -> p f n", p=P)
+        for f in range(0, FEATURE_BLOCKS, 2):
+            nc.sync.dma_start(base_tile[:, f : f + 2, :], base_blocks[:, f : f + 2, :])
         nc.sync.dma_start(w2_tile[:], w2[0])
         nc.sync.dma_start(offsets[:], offs)
         nc.scalar.dma_start(bias[:], b)

import concourse.mybir as mybir
from concourse.masks import make_identity

BF16, F32, U16 = mybir.dt.bfloat16, mybir.dt.float32, mybir.dt.uint16
GELU_TANH = mybir.ActivationFunctionType.Gelu_apprx_tanh

P = 128
K, H, M, N = 256, 128, 512, 256
FEATURE_BLOCKS = M // P
K_BLOCKS = K // P
WARM_UP_COLUMNS = 256
WARM_UP_MATMULS = 8

FLOPS = 2 * K * H * N + 2 * H * M * N


def tile_rows_ffnback_gelu_kernel(tc, base, x, w, b, w2, offs, out):
    nc = tc.nc
    with (
        tc.tile_pool(name="held", bufs=1) as held,
        tc.psum_pool(name="psum", bufs=1) as psum,
    ):
        x_tile = held.tile([P, K_BLOCKS * N], BF16)
        w_tile = held.tile([P, K_BLOCKS * H], BF16)
        bias = held.tile([P, 1], F32)
        base_tile = held.tile([P, FEATURE_BLOCKS, N], BF16)
        offsets = held.tile([P, N // 16], U16)
        w2_tile = held.tile([P, M], BF16)
        nc.sync.dma_start(x_tile[:], x.rearrange("(p a) n -> p (a n)", a=K_BLOCKS))
        nc.sync.dma_start(w_tile[:], w[0].rearrange("(p a) h -> p (a h)", a=K_BLOCKS))
        base_blocks = base.rearrange("(f p) n -> p f n", p=P)
        for f in range(0, FEATURE_BLOCKS, 2):
            nc.sync.dma_start(base_tile[:, f : f + 2, :], base_blocks[:, f : f + 2, :])
        nc.sync.dma_start(w2_tile[:], w2[0])
        nc.sync.dma_start(offsets[:], offs)
        nc.scalar.dma_start(bias[:], b)

        zeros = held.tile([P, WARM_UP_COLUMNS], BF16)
        nc.vector.memset(zeros[:], 0.0)
        gelu_of_zero = held.tile([P, 1], BF16)
        nc.scalar.activation(gelu_of_zero[:], zeros[:, 0:1], GELU_TANH)
        warm_up = psum.tile([P, WARM_UP_COLUMNS], F32)
        for unused in range(WARM_UP_MATMULS):
            nc.tensor.matmul(warm_up[:], zeros[:, 0:P], zeros[:], start=True, stop=True)

        identity = held.tile([P, P], BF16)
        make_identity(nc, identity[:])

        hidden_sum = psum.tile([P, N], F32)
        for a in range(K_BLOCKS):
            nc.tensor.matmul(
                hidden_sum[:],
                w_tile[:, a * H : (a + 1) * H],
                x_tile[:, a * N : (a + 1) * N],
                start=a == 0,
                stop=a == K_BLOCKS - 1,
            )
        hidden = held.tile([P, N], BF16)
        nc.scalar.activation(hidden[:], hidden_sum[:], GELU_TANH, bias=bias[:])

        windows = [psum.tile([P, N], F32, name=f"window{f}") for f in range(FEATURE_BLOCKS)]
        for f in range(FEATURE_BLOCKS):
            nc.tensor.matmul(windows[f][:], identity[:], base_tile[:, f, :], start=True, stop=False)

        for f in range(FEATURE_BLOCKS):
            nc.tensor.matmul(
                windows[f][:].indirect(offsets[:]),
                w2_tile[:, f * P : (f + 1) * P],
                hidden[:],
                start=False,
                stop=True,
            )

        for f in range(FEATURE_BLOCKS):
            result = held.tile([P, N], F32, name=f"result{f}")
            if f % 2 == 0:
                nc.vector.tensor_copy(result[:], windows[f][:])
            else:
                nc.scalar.copy(result[:], windows[f][:])
            nc.sync.dma_start(out[f * P : (f + 1) * P, :], result[:])
